import numpy as np, ml_dtypes
CORES = [10,26,42,58,74,162,290,418]
N = 8
import mx_ref
NC, KB = 128, 1
BF = ml_dtypes.bfloat16
def cut(t, i, w=512):
    return t[:, w * i:w * i + w]
def term(a, B):
    return np.stack([mx_ref.matmul(mx_ref.quantize(cut(a, i)), B) for i in range(4)], axis=2).reshape(128, -1)
def setup_inputs(rng):
    def f(*shape):
        return mx_ref.flush((rng.standard_normal(shape, dtype=np.float32) * np.exp2(rng.integers(-2, 3, shape[:-1] + (1,)))).astype(BF))
    return {"a": f(N, 128, 4 * 512), "b": f(N, 128, KB * 4 * NC)}
def setup_inputs_blocks(rng):
    d = setup_inputs(rng)
    for k in ("a", "b"): d[k] = mx_ref.spread(d[k], rng, 2)
    return d
def setup_inputs_wide(rng):
    d = setup_inputs(rng)
    for k in ("a", "b"): d[k] = mx_ref.flush((d[k].astype(np.float32) * np.exp2(rng.integers(-4, 5, (N, 1, 1))).astype(np.float32)).astype(BF))
    return d
def setup_inputs_lossless(rng):
    a = np.zeros((N, 128, 4 * 128, 4), np.float32)
    for r in range(N):
        k = rng.integers(0, 512, size=4 * 128)
        a[r, k // 4, np.arange(4 * 128), k % 4] = 1.0
    size = np.repeat(2.0 ** rng.integers(-4, 5, size=(1, 1, (KB * 4 * NC) // 4)), 4, axis=2)
    b = rng.integers(-1, 2, size=(N, 128, KB * 4 * NC)) * size
    return {"a": a.reshape(N, 128, 4 * 512).astype(BF), "b": b.astype(np.float32).astype(BF)}
def reference(a, b):
    y = np.zeros((N, 128, KB * 4 * NC), np.float32)
    for k in range(KB):
        y[:, :, 4 * NC * k:4 * NC * k + 4 * NC] = mx_ref.total([term(a[r], mx_ref.quantize(cut(b[r], k, 4 * NC))) for r in range(N)])
    return {"y": y}

@@ -1,0 +1,209 @@
+import numpy as np
+from concourse.bass import DstId, RemoteDMATransfer
+from concourse.mybir import dt, AluOpType, ActivationFunctionType
+
+MSGS = ["t%d" % r for r in range(8)] + ["s", "v", "p"]
+NL = 72
+SCRATCH = {
+    "at": ("sbuf", [128, 2048], "bfloat16"),
+    "bt": ("sbuf", [128, 512], "bfloat16"),
+    "qa": ("sbuf", [128, 512], "float8_e4m3fn_x4"),
+    "sa": ("sbuf", [128, 512], "uint8"),
+    "qb": ("sbuf", [128, 128], "float8_e4m3fn_x4"),
+    "sb": ("sbuf", [128, 128], "uint8"),
+    "ones": ("sbuf", [128, 128], "bfloat16"),
+    "idn": ("sbuf", [128, 128], "bfloat16"),
+    "sel": ("sbuf", [128, 2048], "bfloat16"),
+    "qe": ("sbuf", [128, 512], "float8_e4m3fn_x4"),
+    "se": ("sbuf", [128, 512], "uint8"),
+    "ts0": ("sbuf", [128, 512], "bfloat16"),
+    "ts1": ("sbuf", [128, 512], "bfloat16"),
+    "yo": ("sbuf", [128, 512], "float32"),
+    "acc": ("psum", [128, 2048], "float32"),
+    "mid": ("psum", [128, 2048], "float32"),
+}
+for _m in MSGS:
+    SCRATCH["c_" + _m] = ("sbuf", [128, 128], "float8_e4m3fn_x4")
+    SCRATCH["k_" + _m] = ("sbuf", [128, 128], "uint8")
+SEMAPHORES = (["c_" + m for m in MSGS] + ["k_" + m for m in MSGS] + ["sent"] + ["l%d" % i for i in range(NL)])
+COPY = ActivationFunctionType.Copy
+
+
+def roles(T, topo):
+    cores = T.cores
+    n = len(cores)
+    same = lambda i: [j for j in range(n) if topo.host(cores[j]) == topo.host(cores[i])]
+    loc = max((same(i) for i in range(n)), key=len)
+    h = topo.host(cores[loc[0]])
+    far = [i for i in range(n) if i not in loc]
+    diag = [i for i in far if not topo.may_write(cores[i], cores[loc[0]])][0]
+    near = [i for i in far if i != diag and topo.rack(topo.host(cores[i])) == topo.rack(h)][0]
+    cable = [i for i in far if i not in (diag, near)][0]
+    door = [c for c in range(512) if topo.host(c) == h and topo.chip(c) == topo.chip(cores[cable])][0]
+    mix = [i for i in loc if topo.mates(cores[i], door)][0]
+    p1, p2, hub, fifth = [i for i in loc if i != mix]
+    return loc, near, diag, cable, mix, hub, p1, p2, fifth
+
+
+def rank_program(g, core, T, topo):
+    rank = T.rank_of(core)
+    if rank is None:
+        return
+    loc, near, diag, cable, mix, hub, p1, p2, fifth = roles(T, topo)
+    nl = [0]
+
+    def sem():
+        nl[0] += 1
+        return T.sem["l%d" % (nl[0] - 1)]
+
+    ld = {}
+    for q, name, i in ((g.sync, "b", 0), (g.scalar, "a", 0), (g.sync, "a", 1), (g.scalar, "a", 2), (g.sync, "a", 3)):
+        s = sem()
+        ld[(name, i)] = s
+        if name == "b":
+            q.dma_start(T.bt[:], T.b[:]).then_inc(s, 16)
+        else:
+            q.dma_start(T.at[:, 512 * i:512 * i + 512], T.a[:, 512 * i:512 * i + 512]).then_inc(s, 16)
+
+    s_ones, s_idn, s_zero, s_sel = sem(), sem(), sem(), sem()
+    g.vector.memset(T.ones[:], 1.0).then_inc(s_ones, 1)
+    g.vector.memset(T.sel[:], 0.0).then_inc(s_zero, 1)
+    g.wait_ge(s_ones, 1)
+    g.affine_select(T.idn[:], T.ones[:], [[-1, 128]], AluOpType.is_equal, 0.0, 0, 1).then_inc(s_idn, 1)
+    g.vector.wait_ge(s_idn, 1)
+    g.vector.wait_ge(s_zero, 1)
+    for i in range(4):
+        g.vector.tensor_copy(T.sel[:, 512 * i + i:512 * i + 512:4], T.idn[:]).then_inc(s_sel, 1)
+
+    s_qb, s_qa = sem(), [sem() for _ in range(4)]
+    g.vector.wait_ge(ld[("b", 0)], 16)
+    g.vector.quantize_mx(T.qb[:], T.sb[:], T.bt[:]).then_inc(s_qb, 1)
+    for i in range(4):
+        g.vector.wait_ge(ld[("a", i)], 16)
+        g.vector.quantize_mx(T.qa[:, 128 * i:128 * i + 128], T.sa[:, 128 * i:128 * i + 128],
+                             T.at[:, 512 * i:512 * i + 512]).then_inc(s_qa[i], 1)
+    bank = lambda P, i: P[:, 512 * i:512 * i + 128]
+
+    def product(P, i, stop):
+        return g.tensor.matmul_mx(bank(P, i), T.qa[:, 128 * i:128 * i + 128], T.sa[:, 128 * i:128 * i + 128],
+                                  T.qb[:], T.sb[:], True, stop)
+
+    def decode(P, msgs, fresh):
+        done = [sem() for _ in range(4)]
+        for k, m in enumerate(msgs):
+            if m in ready:
+                g.tensor.wait_ge(ready[m], 1)
+            else:
+                g.tensor.wait_ge(T.sem["c_" + m], 8)
+                g.tensor.wait_ge(T.sem["k_" + m], 8)
+            last = k == len(msgs) - 1
+            for i in range(4):
+                c = g.tensor.matmul_mx(bank(P, i), T.qe[:, 128 * i:128 * i + 128], T.se[:, 128 * i:128 * i + 128],
+                                       T["c_" + m][:], T["k_" + m][:], fresh and k == 0, last)
+                if last:
+                    c.then_inc(done[i], 1)
+        return done
+
+    def drain(out, P, done, on_scalar):
+        s_v, s_s = sem(), sem()
+        for i in range(4):
+            dst = out[:, i:512:4]
+            if i in on_scalar:
+                g.scalar.wait_ge(done[i], 1)
+                g.scalar.activation(dst, bank(P, i), COPY).then_inc(s_s, 1)
+            else:
+                g.vector.wait_ge(done[i], 1)
+                g.vector.tensor_copy(dst, bank(P, i)).then_inc(s_v, 1)
+        return s_v, s_s
+
+    def emit(m, out, P, done, on_scalar):
+        s_v, s_s = drain(out, P, done, on_scalar)
+        g.vector.wait_ge(s_v, 2)
+        g.vector.wait_ge(s_s, 2)
+        s_q = sem()
+        g.vector.quantize_mx(T["c_" + m][:], T["k_" + m][:], out[:]).then_inc(s_q, 1)
+        ready[m] = s_q
+
+    mine, far = "t%d" % rank, "t%d" % cable
+    tl = ["t%d" % r for r in loc if r != rank]
+    passed, final = {
+        hub: ((tl, "s"), ["s", far, "p"]),
+        mix: ((tl + [far], "v"), ["v", "p"]),
+        p1: (None, ["p", "v"]),
+        p2: (None, ["p", "v"]),
+        fifth: (None, ["v", "p"]),
+        near: ((["t%d" % diag], "p"), ["p", far, "s"]),
+        diag: ((["t%d" % near], "p"), ["p", far, "s"]),
+        cable: (None, [mine, "p", "s"]),
+    }[rank]
+
+    ready = {}
+    done = [sem() for _ in range(4)]
+    g.tensor.wait_ge(s_qb, 1)
+    for i in range(4):
+        g.tensor.wait_ge(s_qa[i], 1)
+        product(T.acc, i, True).then_inc(done[i], 1)
+    if passed:
+        for i in range(4):
+            product(T.mid, i, False)
+    emit(mine, T.ts0, T.acc, done, (0, 1))
+    s_qe = sem()
+    g.vector.wait_ge(s_sel, 4)
+    g.vector.quantize_mx(T.qe[:], T.se[:], T.sel[:]).then_inc(s_qe, 1)
+    g.tensor.wait_ge(s_qe, 1)
+    if passed:
+        msgs, m = passed
+        emit(m, T.ts1, T.mid, decode(T.mid, msgs, False), (0, 2))
+    g.tensor.wait_ge(ready[mine], 1)
+    s_v, s_s = drain(T.yo, T.acc, decode(T.acc, final, True), (0, 2))
+    s_y = sem()
+    g.sync.wait_ge(s_v, 2)
+    g.sync.wait_ge(s_s, 2)
+    g.sync.dma_start(T.y[:], T.yo[:]).then_inc(s_y, 16)
+    g.sync.wait_ge(s_y, 16)
+
+    sent = [0]
+    waited = set()
+
+    def send(m, to):
+        dst = [T.cores[r] for r in to]
+        mask = 0xFFFF
+        for d in dst:
+            mask &= topo.mask(core, d)
+        for kind in ("c_", "k_"):
+            key = m if m in ready else kind + m
+            if key not in waited:
+                waited.add(key)
+                if m in ready:
+                    g.wait_ge(ready[m], 1)
+                else:
+                    g.wait_ge(T.sem[kind + m], 8)
+            ap = T[kind + m][:].bitcast(dt.uint8) if kind == "c_" else T[kind + m][:]
+            if len(dst) == 1:
+                rid, pid = topo.addr(dst[0], core)
+                g.remote_dma(ap, ap, T.sem[kind + m], T.sem.sent, pid, rid, mask)
+            else:
+                ids = []
+                for d in dst:
+                    rid, pid = topo.addr(d, core)
+                    ids.append(DstId(rid=rid, pnc=pid))
+                g.remote_dma_fused([RemoteDMATransfer(dst_ids=ids, dma_engine_mask=mask, remote_sem=T.sem[kind + m],
+                                                      srcs=[ap], dsts=[ap] * len(ids), alu_op=0)], local_sem=T.sem.sent)
+            sent[0] += bin(mask).count("1")
+
+    if rank in loc:
+        for r in (hub, mix):
+            if r != rank:
+                send(mine, [r])
+    for m, to in {
+        hub: (("s", [near]), ("s", [cable])),
+        mix: (("v", [fifth, p1, p2]), (far, [hub])),
+        p1: (("p", [hub]),),
+        p2: (("p", [fifth, mix]),),
+        fifth: (),
+        near: ((mine, [diag]), ("p", [p2]), ("p", [p1]), ("s", [diag])),
+        diag: ((mine, [near]), ("p", [cable]), (far, [near])),
+        cable: ((mine, [mix]), (mine, [diag])),
+    }[rank]:
+        send(m, to)
+    g.wait_ge(T.sem.sent, sent[0])

@@ -4,28 +4,23 @@ from concourse.mybir import dt, AluOpType, ActivationFunctionType
 
 MSGS = ["t%d" % r for r in range(8)] + ["s", "v", "p"]
 NL = 72
+BF, F8, U8 = "bfloat16", "float8_e4m3fn_x4", "uint8"
 SCRATCH = {
-    "at": ("sbuf", [128, 2048], "bfloat16"),
-    "bt": ("sbuf", [128, 512], "bfloat16"),
-    "qa": ("sbuf", [128, 512], "float8_e4m3fn_x4"),
-    "sa": ("sbuf", [128, 512], "uint8"),
-    "qb": ("sbuf", [128, 128], "float8_e4m3fn_x4"),
-    "sb": ("sbuf", [128, 128], "uint8"),
-    "ones": ("sbuf", [128, 128], "bfloat16"),
-    "idn": ("sbuf", [128, 128], "bfloat16"),
-    "sel": ("sbuf", [128, 2048], "bfloat16"),
-    "qe": ("sbuf", [128, 512], "float8_e4m3fn_x4"),
-    "se": ("sbuf", [128, 512], "uint8"),
-    "ts0": ("sbuf", [128, 512], "bfloat16"),
-    "ts1": ("sbuf", [128, 512], "bfloat16"),
+    "at": ("sbuf", [128, 2048], BF), "bt": ("sbuf", [128, 512], BF),
+    "qa": ("sbuf", [128, 512], F8), "ka": ("sbuf", [128, 512], U8),
+    "qb": ("sbuf", [128, 128], F8), "kb": ("sbuf", [128, 128], U8),
+    "ones": ("sbuf", [128, 128], BF), "idn": ("sbuf", [128, 128], BF), "sel": ("sbuf", [128, 2048], BF),
+    "qe": ("sbuf", [128, 512], F8), "ke": ("sbuf", [128, 512], U8),
+    "ts0": ("sbuf", [128, 512], BF), "ts1": ("sbuf", [128, 512], BF),
+    "c_half": ("sbuf", [128, 128], F8), "k_half": ("sbuf", [128, 128], U8),
     "yo": ("sbuf", [128, 512], "float32"),
-    "acc": ("psum", [128, 2048], "float32"),
-    "mid": ("psum", [128, 2048], "float32"),
+    "acc": ("psum", [128, 2048], "float32"), "mid": ("psum", [128, 2048], "float32"),
 }
 for _m in MSGS:
-    SCRATCH["c_" + _m] = ("sbuf", [128, 128], "float8_e4m3fn_x4")
-    SCRATCH["k_" + _m] = ("sbuf", [128, 128], "uint8")
-SEMAPHORES = (["c_" + m for m in MSGS] + ["k_" + m for m in MSGS] + ["sent"] + ["l%d" % i for i in range(NL)])
+    SCRATCH["c_" + _m] = ("sbuf", [128, 128], F8)
+    SCRATCH["k_" + _m] = ("sbuf", [128, 128], U8)
+SEMAPHORES = ([k + h + m for k in "ck" for h in "w01" for m in MSGS] + ["sent"] + ["l%d" % i for i in range(NL)])
+COLS = {"w": (0, 128), "0": (0, 64), "1": (64, 128)}
 COPY = ActivationFunctionType.Copy
 
 
@@ -50,160 +45,192 @@ def rank_program(g, core, T, topo):
     if rank is None:
         return
     loc, near, diag, cable, mix, hub, p1, p2, fifth = roles(T, topo)
+    t = lambda r: "t%d" % r
+    far = t(cable)
+    sends = {r: [] for r in range(len(T.cores))}
+
+    def say(r, kinds, m, h, *to):
+        sends[r].extend((k, m, h, to) for k in kinds)
+
+    for r in loc:
+        if r != hub:
+            say(r, "ck", t(r), "0", hub)
+            say(r, "ck", t(r), "1", hub)
+        if r != mix:
+            say(r, "ck", t(r), "w", mix)
+    say(hub, "c", "s", "0", near)
+    say(hub, "k", "s", "w", near)
+    say(hub, "c", "s", "1", cable)
+    say(hub, "k", "s", "w", cable)
+    say(hub, "c", "s", "1", near)
+    say(hub, "c", "s", "0", cable)
+    say(mix, "ck", far, "w", hub)
+    say(mix, "ck", "v", "w", fifth, p1, p2)
+    say(p2, "ck", "p", "w", fifth, mix)
+    say(p1, "ck", "p", "w", hub)
+    say(near, "ck", t(near), "0", diag)
+    say(near, "ck", t(near), "1", diag)
+    say(near, "ck", "p", "w", p2)
+    say(near, "ck", "p", "w", p1)
+    say(near, "c", "s", "0", diag)
+    say(near, "k", "s", "w", diag)
+    say(diag, "ck", t(diag), "0", near)
+    say(diag, "ck", t(diag), "1", near)
+    say(diag, "ck", "p", "w", cable)
+    say(diag, "ck", far, "w", near)
+    say(cable, "ck", far, "0", mix)
+    say(cable, "ck", far, "1", mix)
+    say(cable, "ck", far, "w", diag)
+    say(cable, "c", "s", "1", diag)
+    arrives = {}
+    for r in sends:
+        for k, m, h, to in sends[r]:
+            if rank in to:
+                arrives.setdefault(k + m, []).append(h)
+    mine = t(rank)
+    passed, final = {
+        hub: (([mine] + [t(r) for r in loc if r != hub], "s"), ["s", far, "p"]),
+        mix: (([mine] + [t(r) for r in loc if r != mix] + [far], "v"), ["v", "p"]),
+        p1: (None, ["p", "v"]),
+        p2: (None, ["p", "v"]),
+        fifth: (None, ["v", "p"]),
+        near: (([mine, t(diag)], "p"), ["p", far, "s"]),
+        diag: (([mine, t(near)], "p"), ["p", far, "s"]),
+        cable: (None, [mine, "p", "s"]),
+    }[rank]
     nl = [0]
 
     def sem():
         nl[0] += 1
         return T.sem["l%d" % (nl[0] - 1)]
 
-    ld = {}
-    for q, name, i in ((g.sync, "b", 0), (g.scalar, "a", 0), (g.sync, "a", 1), (g.scalar, "a", 2), (g.sync, "a", 3)):
-        s = sem()
-        ld[(name, i)] = s
-        if name == "b":
-            q.dma_start(T.bt[:], T.b[:]).then_inc(s, 16)
-        else:
-            q.dma_start(T.at[:, 512 * i:512 * i + 512], T.a[:, 512 * i:512 * i + 512]).then_inc(s, 16)
-
-    s_ones, s_idn, s_zero, s_sel = sem(), sem(), sem(), sem()
+    s_b, s_a = sem(), [sem() for _ in range(3)]
+    g.scalar.dma_start(T.at[:, 0:1024], T.a[:, 0:1024]).then_inc(s_a[0], 16)
+    g.sync.dma_start(T.bt[:], T.b[:]).then_inc(s_b, 16)
+    g.sync.dma_start(T.at[:, 1024:1536], T.a[:, 1024:1536]).then_inc(s_a[1], 16)
+    g.sync.dma_start(T.at[:, 1536:2048], T.a[:, 1536:2048]).then_inc(s_a[2], 16)
+    s_ones, s_idn, s_zero, s_sel, s_pad = sem(), sem(), sem(), sem(), sem()
     g.vector.memset(T.ones[:], 1.0).then_inc(s_ones, 1)
     g.vector.memset(T.sel[:], 0.0).then_inc(s_zero, 1)
+    g.vector.memset(T.ts0[:, 256:512], 0.0).then_inc(s_pad, 1)
     g.wait_ge(s_ones, 1)
     g.affine_select(T.idn[:], T.ones[:], [[-1, 128]], AluOpType.is_equal, 0.0, 0, 1).then_inc(s_idn, 1)
     g.vector.wait_ge(s_idn, 1)
     g.vector.wait_ge(s_zero, 1)
     for i in range(4):
         g.vector.tensor_copy(T.sel[:, 512 * i + i:512 * i + 512:4], T.idn[:]).then_inc(s_sel, 1)
-
-    s_qb, s_qa = sem(), [sem() for _ in range(4)]
-    g.vector.wait_ge(ld[("b", 0)], 16)
-    g.vector.quantize_mx(T.qb[:], T.sb[:], T.bt[:]).then_inc(s_qb, 1)
-    for i in range(4):
-        g.vector.wait_ge(ld[("a", i)], 16)
-        g.vector.quantize_mx(T.qa[:, 128 * i:128 * i + 128], T.sa[:, 128 * i:128 * i + 128],
-                             T.at[:, 512 * i:512 * i + 512]).then_inc(s_qa[i], 1)
     bank = lambda P, i: P[:, 512 * i:512 * i + 128]
+    ready = {}
+    s_qb = sem()
+    g.vector.wait_ge(s_b, 16)
+    g.vector.quantize_mx(T.qb[:], T.kb[:], T.bt[:]).then_inc(s_qb, 1)
+    g.tensor.wait_ge(s_qb, 1)
+    for h in range(2):
+        s_mm = []
+        for i in (2 * h, 2 * h + 1):
+            if i != 1:
+                g.vector.wait_ge(s_a[max(i - 1, 0)], 16)
+            s_q, s_m = sem(), sem()
+            w = slice(128 * i, 128 * i + 128)
+            g.vector.quantize_mx(T.qa[:, w], T.ka[:, w], T.at[:, 512 * i:512 * i + 512]).then_inc(s_q, 1)
+            g.tensor.wait_ge(s_q, 1)
+            g.tensor.matmul_mx(bank(T.acc, i), T.qa[:, w], T.ka[:, w], T.qb[:], T.kb[:], True, True).then_inc(s_m, 1)
+            s_mm.append(s_m)
+        s_s, s_v, s_t = sem(), sem(), sem()
+        if h == 0:
+            g.vector.wait_ge(s_pad, 1)
+        else:
+            g.scalar.wait_ge(ready["half"], 1)
+            g.vector.wait_ge(ready["half"], 1)
+        g.scalar.wait_ge(s_mm[0], 1)
+        g.scalar.activation(T.ts0[:, 256 * h:256 * h + 256:2], bank(T.acc, 2 * h), COPY).then_inc(s_s, 1)
+        g.vector.wait_ge(s_mm[1], 1)
+        g.vector.tensor_copy(T.ts0[:, 256 * h + 1:256 * h + 256:2], bank(T.acc, 2 * h + 1)).then_inc(s_v, 1)
+        g.vector.wait_ge(s_s, 1)
+        g.vector.wait_ge(s_v, 1)
+        m = mine if h else "half"
+        g.vector.quantize_mx(T["c_" + m][:], T["k_" + m][:], T.ts0[:]).then_inc(s_t, 1)
+        ready[m] = s_t
+    s_qe = sem()
+    g.vector.wait_ge(s_sel, 4)
+    g.vector.quantize_mx(T.qe[:], T.ke[:], T.sel[:]).then_inc(s_qe, 1)
+    g.tensor.wait_ge(s_qe, 1)
 
-    def product(P, i, stop):
-        return g.tensor.matmul_mx(bank(P, i), T.qa[:, 128 * i:128 * i + 128], T.sa[:, 128 * i:128 * i + 128],
-                                  T.qb[:], T.sb[:], True, stop)
-
-    def decode(P, msgs, fresh):
+    def decode(P, msgs):
         done = [sem() for _ in range(4)]
-        for k, m in enumerate(msgs):
+        for j, m in enumerate(msgs):
             if m in ready:
                 g.tensor.wait_ge(ready[m], 1)
             else:
-                g.tensor.wait_ge(T.sem["c_" + m], 8)
-                g.tensor.wait_ge(T.sem["k_" + m], 8)
-            last = k == len(msgs) - 1
+                for k in "ck":
+                    for h in arrives[k + m]:
+                        g.tensor.wait_ge(T.sem[k + h + m], 8)
+            last = j == len(msgs) - 1
             for i in range(4):
-                c = g.tensor.matmul_mx(bank(P, i), T.qe[:, 128 * i:128 * i + 128], T.se[:, 128 * i:128 * i + 128],
-                                       T["c_" + m][:], T["k_" + m][:], fresh and k == 0, last)
+                c = g.tensor.matmul_mx(bank(P, i), T.qe[:, 128 * i:128 * i + 128], T.ke[:, 128 * i:128 * i + 128],
+                                       T["c_" + m][:], T["k_" + m][:], j == 0, last)
                 if last:
                     c.then_inc(done[i], 1)
         return done
 
-    def drain(out, P, done, on_scalar):
-        s_v, s_s = sem(), sem()
-        for i in range(4):
-            dst = out[:, i:512:4]
-            if i in on_scalar:
-                g.scalar.wait_ge(done[i], 1)
-                g.scalar.activation(dst, bank(P, i), COPY).then_inc(s_s, 1)
-            else:
-                g.vector.wait_ge(done[i], 1)
-                g.vector.tensor_copy(dst, bank(P, i)).then_inc(s_v, 1)
-        return s_v, s_s
-
-    def emit(m, out, P, done, on_scalar):
-        s_v, s_s = drain(out, P, done, on_scalar)
-        g.vector.wait_ge(s_v, 2)
-        g.vector.wait_ge(s_s, 2)
-        s_q = sem()
-        g.vector.quantize_mx(T["c_" + m][:], T["k_" + m][:], out[:]).then_inc(s_q, 1)
-        ready[m] = s_q
-
-    mine, far = "t%d" % rank, "t%d" % cable
-    tl = ["t%d" % r for r in loc if r != rank]
-    passed, final = {
-        hub: ((tl, "s"), ["s", far, "p"]),
-        mix: ((tl + [far], "v"), ["v", "p"]),
-        p1: (None, ["p", "v"]),
-        p2: (None, ["p", "v"]),
-        fifth: (None, ["v", "p"]),
-        near: ((["t%d" % diag], "p"), ["p", far, "s"]),
-        diag: ((["t%d" % near], "p"), ["p", far, "s"]),
-        cable: (None, [mine, "p", "s"]),
-    }[rank]
-
-    ready = {}
-    done = [sem() for _ in range(4)]
-    g.tensor.wait_ge(s_qb, 1)
-    for i in range(4):
-        g.tensor.wait_ge(s_qa[i], 1)
-        product(T.acc, i, True).then_inc(done[i], 1)
-    if passed:
-        for i in range(4):
-            product(T.mid, i, False)
-    emit(mine, T.ts0, T.acc, done, (0, 1))
-    s_qe = sem()
-    g.vector.wait_ge(s_sel, 4)
-    g.vector.quantize_mx(T.qe[:], T.se[:], T.sel[:]).then_inc(s_qe, 1)
-    g.tensor.wait_ge(s_qe, 1)
     if passed:
         msgs, m = passed
-        emit(m, T.ts1, T.mid, decode(T.mid, msgs, False), (0, 2))
+        done = decode(T.mid, msgs)
+        s_v, s_s, s_q = sem(), sem(), sem()
+        for i in range(4):
+            q, s = ((g.scalar, s_s), (g.vector, s_v))[i & 1]
+            q.wait_ge(done[i], 1)
+            if i & 1:
+                q.tensor_copy(T.ts1[:, i:512:4], bank(T.mid, i)).then_inc(s, 1)
+            else:
+                q.activation(T.ts1[:, i:512:4], bank(T.mid, i), COPY).then_inc(s, 1)
+        g.vector.wait_ge(s_v, 2)
+        g.vector.wait_ge(s_s, 2)
+        g.vector.quantize_mx(T["c_" + m][:], T["k_" + m][:], T.ts1[:]).then_inc(s_q, 1)
+        ready[m] = s_q
     g.tensor.wait_ge(ready[mine], 1)
-    s_v, s_s = drain(T.yo, T.acc, decode(T.acc, final, True), (0, 2))
-    s_y = sem()
-    g.sync.wait_ge(s_v, 2)
-    g.sync.wait_ge(s_s, 2)
+    done = decode(T.acc, final)
+    s_v, s_s, s_y = sem(), sem(), sem()
+    for i in range(4):
+        q, s = ((g.scalar, s_s), (g.vector, s_v))[i & 1]
+        q.wait_ge(done[i], 1)
+        for h in range(2):
+            j = 4 * (i >> 1) + (i & 1) + 2 * h
+            dst, src = T.yo[:, j:512:8], T.acc[:, 512 * i + 64 * h:512 * i + 64 * h + 64]
+            if i & 1:
+                q.tensor_copy(dst, src).then_inc(s, 1)
+            else:
+                q.activation(dst, src, COPY).then_inc(s, 1)
+    g.sync.wait_ge(s_v, 4)
+    g.sync.wait_ge(s_s, 4)
     g.sync.dma_start(T.y[:], T.yo[:]).then_inc(s_y, 16)
     g.sync.wait_ge(s_y, 16)
 
-    sent = [0]
-    waited = set()
-
-    def send(m, to):
+    sent = 0
+    for k, m, h, to in sends[rank]:
         dst = [T.cores[r] for r in to]
         mask = 0xFFFF
         for d in dst:
             mask &= topo.mask(core, d)
-        for kind in ("c_", "k_"):
-            key = m if m in ready else kind + m
-            if key not in waited:
-                waited.add(key)
-                if m in ready:
-                    g.wait_ge(ready[m], 1)
-                else:
-                    g.wait_ge(T.sem[kind + m], 8)
-            ap = T[kind + m][:].bitcast(dt.uint8) if kind == "c_" else T[kind + m][:]
-            if len(dst) == 1:
-                rid, pid = topo.addr(dst[0], core)
-                g.remote_dma(ap, ap, T.sem[kind + m], T.sem.sent, pid, rid, mask)
-            else:
-                ids = []
-                for d in dst:
-                    rid, pid = topo.addr(d, core)
-                    ids.append(DstId(rid=rid, pnc=pid))
-                g.remote_dma_fused([RemoteDMATransfer(dst_ids=ids, dma_engine_mask=mask, remote_sem=T.sem[kind + m],
-                                                      srcs=[ap], dsts=[ap] * len(ids), alu_op=0)], local_sem=T.sem.sent)
-            sent[0] += bin(mask).count("1")
-
-    if rank in loc:
-        for r in (hub, mix):
-            if r != rank:
-                send(mine, [r])
-    for m, to in {
-        hub: (("s", [near]), ("s", [cable])),
-        mix: (("v", [fifth, p1, p2]), (far, [hub])),
-        p1: (("p", [hub]),),
-        p2: (("p", [fifth, mix]),),
-        fifth: (),
-        near: ((mine, [diag]), ("p", [p2]), ("p", [p1]), ("s", [diag])),
-        diag: ((mine, [near]), ("p", [cable]), (far, [near])),
-        cable: ((mine, [mix]), (mine, [diag])),
-    }[rank]:
-        send(m, to)
-    g.wait_ge(T.sem.sent, sent[0])
+        early = m == mine and h == "0"
+        if early:
+            g.wait_ge(ready["half"], 1)
+        elif m in ready:
+            g.wait_ge(ready[m], 1)
+        else:
+            for piece in (arrives[k + m] if h not in arrives[k + m] else [h]):
+                g.wait_ge(T.sem[k + piece + m], 8)
+        lo, hi = COLS[h]
+        src, out = T[k + ("_half" if early else "_" + m)][:, lo:hi], T[k + "_" + m][:, lo:hi]
+        if k == "c":
+            src, out = src.bitcast(dt.uint8), out.bitcast(dt.uint8)
+        s = T.sem[k + h + m]
+        ids = [topo.addr(d, core) for d in dst]
+        if len(ids) == 1:
+            g.remote_dma(out, src, s, T.sem.sent, ids[0][1], ids[0][0], mask)
+        else:
+            g.remote_dma_fused([RemoteDMATransfer(dst_ids=[DstId(rid=rid, pnc=pid) for rid, pid in ids],
+                                                  dma_engine_mask=mask, remote_sem=s, srcs=[src],
+                                                  dsts=[out] * len(ids), alu_op=0)], local_sem=T.sem.sent)
+        sent += bin(mask).count("1")
+    g.wait_ge(T.sem.sent, sent)

import numpy as np
from concourse.bass import DstId, RemoteDMATransfer
from concourse.mybir import dt, AluOpType, ActivationFunctionType

MSGS = ["t%d" % r for r in range(8)] + ["s", "v", "p"]
NL = 72
BF, F8, U8 = "bfloat16", "float8_e4m3fn_x4", "uint8"
SCRATCH = {
    "at": ("sbuf", [128, 2048], BF), "bt": ("sbuf", [128, 512], BF),
    "qa": ("sbuf", [128, 512], F8), "ka": ("sbuf", [128, 512], U8),
    "qb": ("sbuf", [128, 128], F8), "kb": ("sbuf", [128, 128], U8),
    "ones": ("sbuf", [128, 128], BF), "idn": ("sbuf", [128, 128], BF), "sel": ("sbuf", [128, 2048], BF),
    "qe": ("sbuf", [128, 512], F8), "ke": ("sbuf", [128, 512], U8),
    "ts0": ("sbuf", [128, 512], BF), "ts1": ("sbuf", [128, 512], BF),
    "c_half": ("sbuf", [128, 128], F8), "k_half": ("sbuf", [128, 128], U8),
    "yo": ("sbuf", [128, 512], "float32"),
    "acc": ("psum", [128, 2048], "float32"), "mid": ("psum", [128, 2048], "float32"),
}
for _m in MSGS:
    SCRATCH["c_" + _m] = ("sbuf", [128, 128], F8)
    SCRATCH["k_" + _m] = ("sbuf", [128, 128], U8)
SEMAPHORES = ([k + h + m for k in "ck" for h in "w01" for m in MSGS] + ["sent"] + ["l%d" % i for i in range(NL)])
COLS = {"w": (0, 128), "0": (0, 64), "1": (64, 128)}
COPY = ActivationFunctionType.Copy


def roles(T, topo):
    cores = T.cores
    n = len(cores)
    same = lambda i: [j for j in range(n) if topo.host(cores[j]) == topo.host(cores[i])]
    loc = max((same(i) for i in range(n)), key=len)
    h = topo.host(cores[loc[0]])
    far = [i for i in range(n) if i not in loc]
    diag = [i for i in far if not topo.may_write(cores[i], cores[loc[0]])][0]
    near = [i for i in far if i != diag and topo.rack(topo.host(cores[i])) == topo.rack(h)][0]
    cable = [i for i in far if i not in (diag, near)][0]
    door = [c for c in range(512) if topo.host(c) == h and topo.chip(c) == topo.chip(cores[cable])][0]
    mix = [i for i in loc if topo.mates(cores[i], door)][0]
    p1, p2, hub, fifth = [i for i in loc if i != mix]
    return loc, near, diag, cable, mix, hub, p1, p2, fifth


def rank_program(g, core, T, topo):
    rank = T.rank_of(core)
    if rank is None:
        return
    loc, near, diag, cable, mix, hub, p1, p2, fifth = roles(T, topo)
    t = lambda r: "t%d" % r
    far = t(cable)
    sends = {r: [] for r in range(len(T.cores))}

    def say(r, kinds, m, h, *to):
        sends[r].extend((k, m, h, to) for k in kinds)

    for r in loc:
        if r != hub:
            say(r, "ck", t(r), "0", hub)
            say(r, "ck", t(r), "1", hub)
        if r != mix:
            say(r, "ck", t(r), "w", mix)
    say(hub, "c", "s", "0", near)
    say(hub, "k", "s", "w", near)
    say(hub, "c", "s", "1", cable)
    say(hub, "k", "s", "w", cable)
    say(hub, "c", "s", "1", near)
    say(hub, "c", "s", "0", cable)
    say(mix, "ck", far, "w", hub)
    say(mix, "ck", "v", "w", fifth, p1, p2)
    say(p2, "ck", "p", "w", fifth, mix)
    say(p1, "ck", "p", "w", hub)
    say(near, "ck", t(near), "0", diag)
    say(near, "ck", t(near), "1", diag)
    say(near, "ck", "p", "w", p2)
    say(near, "ck", "p", "w", p1)
    say(near, "c", "s", "0", diag)
    say(near, "k", "s", "w", diag)
    say(diag, "ck", t(diag), "0", near)
    say(diag, "ck", t(diag), "1", near)
    say(diag, "ck", "p", "w", cable)
    say(diag, "ck", far, "w", near)
    say(cable, "ck", far, "0", mix)
    say(cable, "ck", far, "1", mix)
    say(cable, "ck", far, "w", diag)
    say(cable, "c", "s", "1", diag)
    arrives = {}
    for r in sends:
        for k, m, h, to in sends[r]:
            if rank in to:
                arrives.setdefault(k + m, []).append(h)
    mine = t(rank)
    passed, final = {
        hub: (([mine] + [t(r) for r in loc if r != hub], "s"), ["s", far, "p"]),
        mix: (([mine] + [t(r) for r in loc if r != mix] + [far], "v"), ["v", "p"]),
        p1: (None, ["p", "v"]),
        p2: (None, ["p", "v"]),
        fifth: (None, ["v", "p"]),
        near: (([mine, t(diag)], "p"), ["p", far, "s"]),
        diag: (([mine, t(near)], "p"), ["p", far, "s"]),
        cable: (None, [mine, "p", "s"]),
    }[rank]
    nl = [0]

    def sem():
        nl[0] += 1
        return T.sem["l%d" % (nl[0] - 1)]

    s_b, s_a = sem(), [sem() for _ in range(3)]
    g.scalar.dma_start(T.at[:, 0:1024], T.a[:, 0:1024]).then_inc(s_a[0], 16)
    g.sync.dma_start(T.bt[:], T.b[:]).then_inc(s_b, 16)
    g.sync.dma_start(T.at[:, 1024:1536], T.a[:, 1024:1536]).then_inc(s_a[1], 16)
    g.sync.dma_start(T.at[:, 1536:2048], T.a[:, 1536:2048]).then_inc(s_a[2], 16)
    s_ones, s_idn, s_zero, s_sel, s_pad = sem(), sem(), sem(), sem(), sem()
    g.vector.memset(T.ones[:], 1.0).then_inc(s_ones, 1)
    g.vector.memset(T.sel[:], 0.0).then_inc(s_zero, 1)
    g.vector.memset(T.ts0[:, 256:512], 0.0).then_inc(s_pad, 1)
    g.wait_ge(s_ones, 1)
    g.affine_select(T.idn[:], T.ones[:], [[-1, 128]], AluOpType.is_equal, 0.0, 0, 1).then_inc(s_idn, 1)
    g.vector.wait_ge(s_idn, 1)
    g.vector.wait_ge(s_zero, 1)
    for i in range(4):
        g.vector.tensor_copy(T.sel[:, 512 * i + i:512 * i + 512:4], T.idn[:]).then_inc(s_sel, 1)
    bank = lambda P, i: P[:, 512 * i:512 * i + 128]
    ready = {}
    s_qb = sem()
    g.vector.wait_ge(s_b, 16)
    g.vector.quantize_mx(T.qb[:], T.kb[:], T.bt[:]).then_inc(s_qb, 1)
    g.tensor.wait_ge(s_qb, 1)
    for h in range(2):
        s_mm = []
        for i in (2 * h, 2 * h + 1):
            if i != 1:
                g.vector.wait_ge(s_a[max(i - 1, 0)], 16)
            s_q, s_m = sem(), sem()
            w = slice(128 * i, 128 * i + 128)
            g.vector.quantize_mx(T.qa[:, w], T.ka[:, w], T.at[:, 512 * i:512 * i + 512]).then_inc(s_q, 1)
            g.tensor.wait_ge(s_q, 1)
            g.tensor.matmul_mx(bank(T.acc, i), T.qa[:, w], T.ka[:, w], T.qb[:], T.kb[:], True, True).then_inc(s_m, 1)
            s_mm.append(s_m)
        s_s, s_v, s_t = sem(), sem(), sem()
        if h == 0:
            g.vector.wait_ge(s_pad, 1)
        else:
            g.scalar.wait_ge(ready["half"], 1)
            g.vector.wait_ge(ready["half"], 1)
        g.scalar.wait_ge(s_mm[0], 1)
        g.scalar.activation(T.ts0[:, 256 * h:256 * h + 256:2], bank(T.acc, 2 * h), COPY).then_inc(s_s, 1)
        g.vector.wait_ge(s_mm[1], 1)
        g.vector.tensor_copy(T.ts0[:, 256 * h + 1:256 * h + 256:2], bank(T.acc, 2 * h + 1)).then_inc(s_v, 1)
        g.vector.wait_ge(s_s, 1)
        g.vector.wait_ge(s_v, 1)
        m = mine if h else "half"
        g.vector.quantize_mx(T["c_" + m][:], T["k_" + m][:], T.ts0[:]).then_inc(s_t, 1)
        ready[m] = s_t
    s_qe = sem()
    g.vector.wait_ge(s_sel, 4)
    g.vector.quantize_mx(T.qe[:], T.ke[:], T.sel[:]).then_inc(s_qe, 1)
    g.tensor.wait_ge(s_qe, 1)

    def decode(P, msgs):
        done = [sem() for _ in range(4)]
        for j, m in enumerate(msgs):
            if m in ready:
                g.tensor.wait_ge(ready[m], 1)
            else:
                for k in "ck":
                    for h in arrives[k + m]:
                        g.tensor.wait_ge(T.sem[k + h + m], 8)
            last = j == len(msgs) - 1
            for i in range(4):
                c = g.tensor.matmul_mx(bank(P, i), T.qe[:, 128 * i:128 * i + 128], T.ke[:, 128 * i:128 * i + 128],
                                       T["c_" + m][:], T["k_" + m][:], j == 0, last)
                if last:
                    c.then_inc(done[i], 1)
        return done

    if passed:
        msgs, m = passed
        done = decode(T.mid, msgs)
        s_v, s_s, s_q = sem(), sem(), sem()
        for i in range(4):
            q, s = ((g.scalar, s_s), (g.vector, s_v))[i & 1]
            q.wait_ge(done[i], 1)
            if i & 1:
                q.tensor_copy(T.ts1[:, i:512:4], bank(T.mid, i)).then_inc(s, 1)
            else:
                q.activation(T.ts1[:, i:512:4], bank(T.mid, i), COPY).then_inc(s, 1)
        g.vector.wait_ge(s_v, 2)
        g.vector.wait_ge(s_s, 2)
        g.vector.quantize_mx(T["c_" + m][:], T["k_" + m][:], T.ts1[:]).then_inc(s_q, 1)
        ready[m] = s_q
    g.tensor.wait_ge(ready[mine], 1)
    done = decode(T.acc, final)
    s_v, s_s, s_y = sem(), sem(), sem()
    for i in range(4):
        q, s = ((g.scalar, s_s), (g.vector, s_v))[i & 1]
        q.wait_ge(done[i], 1)
        for h in range(2):
            j = 4 * (i >> 1) + (i & 1) + 2 * h
            dst, src = T.yo[:, j:512:8], T.acc[:, 512 * i + 64 * h:512 * i + 64 * h + 64]
            if i & 1:
                q.tensor_copy(dst, src).then_inc(s, 1)
            else:
                q.activation(dst, src, COPY).then_inc(s, 1)
    g.sync.wait_ge(s_v, 4)
    g.sync.wait_ge(s_s, 4)
    g.sync.dma_start(T.y[:], T.yo[:]).then_inc(s_y, 16)
    g.sync.wait_ge(s_y, 16)

    sent = 0
    for k, m, h, to in sends[rank]:
        dst = [T.cores[r] for r in to]
        mask = 0xFFFF
        for d in dst:
            mask &= topo.mask(core, d)
        early = m == mine and h == "0"
        if early:
            g.wait_ge(ready["half"], 1)
        elif m in ready:
            g.wait_ge(ready[m], 1)
        else:
            for piece in (arrives[k + m] if h not in arrives[k + m] else [h]):
                g.wait_ge(T.sem[k + piece + m], 8)
        lo, hi = COLS[h]
        src, out = T[k + ("_half" if early else "_" + m)][:, lo:hi], T[k + "_" + m][:, lo:hi]
        if k == "c":
            src, out = src.bitcast(dt.uint8), out.bitcast(dt.uint8)
        s = T.sem[k + h + m]
        ids = [topo.addr(d, core) for d in dst]
        if len(ids) == 1:
            g.remote_dma(out, src, s, T.sem.sent, ids[0][1], ids[0][0], mask)
        else:
            g.remote_dma_fused([RemoteDMATransfer(dst_ids=[DstId(rid=rid, pnc=pid) for rid, pid in ids],
                                                  dma_engine_mask=mask, remote_sem=s, srcs=[src],
                                                  dsts=[out] * len(ids), alu_op=0)], local_sem=T.sem.sent)
        sent += bin(mask).count("1")
    g.wait_ge(T.sem.sent, sent)
